import numpy as np
CORES = [24,40,56,80,88,96]
N = 6
TK = 256
D = 128 * N
EPS = 0.01
def setup_inputs(rng):
    return {"x": (rng.standard_normal((N, 128, TK), dtype=np.float32) * (0.5 + np.abs(rng.standard_normal((1, 1, TK), dtype=np.float32))) + rng.standard_normal((1, 1, TK), dtype=np.float32))}
def setup_inputs_big(rng):
    d = setup_inputs(rng)
    for k in ("x",): d[k] = (d[k].astype(np.float32) * 1024.0).astype(d[k].dtype)
    return d
def setup_inputs_small(rng):
    d = setup_inputs(rng)
    for k in ("x",): d[k] = (d[k].astype(np.float32) * (1 / 1024.0)).astype(d[k].dtype)
    return d
def setup_inputs_apart(rng):
    d = setup_inputs(rng)
    f = (10.0 ** rng.permutation(np.linspace(-1.5, 1.5, N))).astype(np.float32).reshape(N, 1, 1)
    for k in ("x",): d[k] = (d[k].astype(np.float32) * f).astype(d[k].dtype)
    return d
def setup_inputs_mixed(rng):
    d = setup_inputs(rng)
    f = (10.0 ** rng.uniform(-3, 3, (1, 1, TK))).astype(np.float32); shape = rng.integers(3, size=(1, 1, TK))
    for k in ("x",):
        x = d[k].astype(np.float32)
        m = x.mean(axis=(0, 1), keepdims=True); level = m + np.sign(x - m) * np.abs(x - m).mean(axis=(0, 1), keepdims=True) * rng.uniform(0.9, 1.1, x.shape).astype(np.float32)
        other = x * np.where(rng.random(x.shape) < 0.5, 0.1, 1.0).astype(np.float32)
        d[k] = (np.where(shape == 1, level, np.where(shape == 2, other, x)) * f).astype(d[k].dtype)
    return d
def reference(x):
    X = x.astype(np.float64)
    Z = X
    Z = Z / np.sqrt((Z ** 2).sum(axis=(0, 1)) / D + EPS)
    return {"y": Z.astype(np.float32)}

@@ -1,0 +1,172 @@
+from concourse.bass import DstId, RemoteDMATransfer
+from concourse.mybir import AluOpType, AxisListType, ActivationFunctionType
+
+N = 6
+TK = 256
+HALF = 128
+D = 128 * N
+EPS = 0.01
+SIM_CORES = 112
+SH = 2.0 ** -22
+C = SH * SH
+SLOT = 4
+
+NH = 2
+E_RANK = 8
+E_RELAY = 8
+
+SCRATCH = {
+    "xs": ("sbuf", [128, TK], "float32"),
+    "sq": ("sbuf", [128, TK], "float32"),
+    "ys": ("sbuf", [128, TK], "float32"),
+    "ones": ("sbuf", [128, 128], "float32"),
+    "shm": ("sbuf", [128, 128], "float32"),
+    "ident": ("sbuf", [128, 128], "float32"),
+    "diag": ("sbuf", [128, TK], "float32"),
+    "land": ("sbuf", [128, SLOT * N], "float32"),
+    "tot": ("sbuf", [128, 2], "float32"),
+    "vp": ("sbuf", [128, 2], "float32"),
+    "z": ("sbuf", [128, 6], "float32"),
+    "w": ("sbuf", [128, 6], "float32"),
+    "o": ("sbuf", [128, 6], "float32"),
+    "ps_part": ("psum", [128, 512], "float32"),
+    "ps_a": ("psum", [128, 512], "float32"),
+    "ps_b": ("psum", [128, 512], "float32"),
+}
+SEMAPHORES = ["ld", "cst", "idn", "sq0", "sq1", "mm", "pr", "arr", "sent", "rd", "vq", "sr", "sc0", "sc1",
+              "dg0", "dg1", "bc0", "bc1", "ml0", "ml1", "st"]
+
+
+def _engines(mask, n):
+    out, bit, k = 0, 1, 0
+    while k < n:
+        if mask & bit:
+            out |= bit
+            k += 1
+        bit <<= 1
+    return out
+
+
+def _common_mask(topo, src, dsts, n):
+    m = topo.mask(src, dsts[0])
+    for d in dsts[1:]:
+        m &= topo.mask(src, d)
+    return _engines(m, n)
+
+
+def _plan(T, topo):
+    group = list(T.cores)
+    plan = {}
+    for c in group:
+        direct = [d for d in group if d != c and topo.may_write(c, d)]
+        far = [d for d in group if d != c and not topo.may_write(c, d)]
+        cand = [h for h in range(SIM_CORES)
+                if topo.chip(h) == topo.chip(c) and h not in group and all(topo.may_write(h, d) for d in far)]
+        cand.sort(key=lambda h: (topo.die(h) != topo.die(c), h))
+        nh = min(NH, len(far), len(cand))
+        relays = [(cand[i], far[i::nh]) for i in range(nh)]
+        plan[c] = (direct, relays)
+    return plan
+
+
+def _send(g, T, topo, src_core, dsts, ap, n_eng):
+    ids = []
+    for d in dsts:
+        rid, pid, _se = topo.addr(d)
+        ids.append(DstId(rid=rid, pnc=pid))
+    g.remote_dma_fused(
+        [RemoteDMATransfer(dst_ids=ids, dma_engine_mask=_common_mask(topo, src_core, dsts, n_eng),
+                           remote_sem=T.sem.arr, srcs=[ap], dsts=[ap for _d in dsts], alu_op=0)],
+        local_sem=T.sem.sent)
+
+
+def rank_program(g, core, T, topo):
+    plan = _plan(T, topo)
+    rank = T.rank_of(core)
+    mult, add = AluOpType.mult, AluOpType.add
+
+    if rank is None:
+        for c in plan:
+            for h, share in plan[c][1]:
+                if h == core:
+                    r = T.rank_of(c)
+                    slot = T.land[:, SLOT * r:SLOT * r + 2]
+                    g.wait_ge(T.sem.arr, E_RANK)
+                    _send(g, T, topo, core, share, slot, E_RELAY)
+                    g.wait_ge(T.sem.sent, E_RELAY)
+        return
+
+    direct, relays = plan[core]
+    expected = 0
+    for c in plan:
+        if core in plan[c][0]:
+            expected += E_RANK
+        for _h, share in plan[c][1]:
+            if core in share:
+                expected += E_RELAY
+    mine = T.land[:, SLOT * rank:SLOT * rank + 2]
+    v, a, pe, sy = g.vector, g.scalar, g.tensor, g.sync
+    S = T.sem
+
+    sy.dma_start(T.xs[:], T.x[:]).then_inc(S.ld, 16)
+    v.memset(T.ones[:], 1.0).then_inc(S.cst, 1)
+    v.memset(T.shm[:], SH).then_inc(S.cst, 1)
+    v.memset(T.w[:], 0.0).then_inc(S.cst, 1)
+    g.wait_ge(S.cst, 3)
+    g.affine_select(T.ident[:], T.ones[:], [[-1, 128]], AluOpType.is_equal, 0.0, 0, 1).then_inc(S.idn, 1)
+
+    a.wait_ge(S.ld, 16)
+    a.activation(T.sq[:, 0:HALF], T.xs[:, 0:HALF], ActivationFunctionType.Square, scale=SH).then_inc(S.sq0, 1)
+    a.activation(T.sq[:, HALF:TK], T.xs[:, HALF:TK], ActivationFunctionType.Square, scale=SH).then_inc(S.sq1, 1)
+    pe.wait_ge(S.cst, 3)
+    pe.wait_ge(S.sq0, 1)
+    pe.matmul(T.ps_part[:, 0:1], T.sq[:, 0:HALF], T.ones[:, 0:1], True, True).then_inc(S.mm, 1)
+    pe.wait_ge(S.sq1, 1)
+    pe.matmul(T.ps_part[:, 1:2], T.sq[:, HALF:TK], T.ones[:, 0:1], True, True).then_inc(S.mm, 1)
+    v.wait_ge(S.mm, 2)
+    v.tensor_copy(mine, T.ps_part[:, 0:2]).then_inc(S.pr, 1)
+
+    g.wait_ge(S.pr, 1)
+    _send(g, T, topo, core, [h for h, _s in relays], mine, E_RANK)
+    _send(g, T, topo, core, direct, mine, E_RANK)
+
+    v.wait_ge(S.pr, 1)
+    v.wait_ge(S.arr, expected)
+    v.tensor_reduce(T.tot[:, 0:1], T.land[:, 0:SLOT * N:SLOT], AxisListType.X, add).then_inc(S.rd, 1)
+    v.tensor_reduce(T.tot[:, 1:2], T.land[:, 1:SLOT * N:SLOT], AxisListType.X, add).then_inc(S.rd, 1)
+    a.wait_ge(S.rd, 2)
+    a.activation(T.z[:, 1:6:3], T.tot[:], ActivationFunctionType.Sqrt, bias=EPS * C, scale=1.0 / D).then_inc(S.sr, 1)
+    v.wait_ge(S.rd, 2)
+    v.tensor_scalar(T.vp[:], T.tot[:], 1.0 / D, EPS * C, mult, add).then_inc(S.vq, 1)
+    v.wait_ge(S.vq, 1)
+    v.reciprocal(T.z[:, 0:6:3], T.vp[:]).then_inc(S.vq, 1)
+    v.wait_ge(S.vq, 2)
+    v.tensor_scalar(T.z[:, 2:6:3], T.z[:, 0:6:3], -0.5, None, mult).then_inc(S.vq, 1)
+    v.tensor_scalar(T.w[:, 2:6:3], T.z[:, 0:6:3], 1.5, None, mult).then_inc(S.vq, 1)
+    v.wait_ge(S.vq, 4)
+    v.wait_ge(S.cst, 3)
+    v.wait_ge(S.idn, 1)
+    v.wait_ge(S.ld, 16)
+    v.wait_ge(S.sr, 1)
+    v.tensor_tensor_scan(T.o[:, 0:3], T.z[:, 0:3], T.w[:, 0:3], T.z[:, 1:2], mult, add).then_inc(S.sc0, 1)
+    v.wait_ge(S.sc0, 1)
+    v.tensor_scalar(T.diag[:, 0:HALF], T.ident[:], T.z[:, 1:2], T.o[:, 2:3], mult, mult).then_inc(S.dg0, 1)
+    v.tensor_tensor_scan(T.o[:, 3:6], T.z[:, 3:6], T.w[:, 3:6], T.z[:, 4:5], mult, add).then_inc(S.sc1, 1)
+    v.wait_ge(S.sc1, 1)
+    v.tensor_scalar(T.diag[:, HALF:TK], T.ident[:], T.z[:, 4:5], T.o[:, 5:6], mult, mult).then_inc(S.dg1, 1)
+
+    pe.wait_ge(S.dg0, 1)
+    pe.matmul(T.ps_a[:, 0:HALF], T.shm[:], T.diag[:, 0:HALF], True, True).then_inc(S.bc0, 1)
+    pe.wait_ge(S.dg1, 1)
+    pe.matmul(T.ps_b[:, 0:HALF], T.shm[:], T.diag[:, HALF:TK], True, True).then_inc(S.bc1, 1)
+    v.wait_ge(S.bc0, 1)
+    v.tensor_tensor(T.ys[:, 0:HALF], T.xs[:, 0:HALF], T.ps_a[:, 0:HALF], mult).then_inc(S.ml0, 1)
+    v.wait_ge(S.bc1, 1)
+    v.tensor_tensor(T.ys[:, HALF:TK], T.xs[:, HALF:TK], T.ps_b[:, 0:HALF], mult).then_inc(S.ml1, 1)
+    sy.wait_ge(S.ml0, 1)
+    sy.dma_start(T.y[:, 0:HALF], T.ys[:, 0:HALF]).then_inc(S.st, 16)
+    a.wait_ge(S.ml1, 1)
+    a.dma_start(T.y[:, HALF:TK], T.ys[:, HALF:TK]).then_inc(S.st, 16)
+
+    g.wait_ge(S.sent, 2 * E_RANK)
+    sy.wait_ge(S.st, 32)

@@ -9,6 +9,7 @@ EPS = 0.01
 SIM_CORES = 112
 SH = 2.0 ** -22
 C = SH * SH
+K = 2.0 ** -44
 SLOT = 4
 
 NH = 2
@@ -25,16 +26,26 @@ SCRATCH = {
     "diag": ("sbuf", [128, TK], "float32"),
     "land": ("sbuf", [128, SLOT * N], "float32"),
     "tot": ("sbuf", [128, 2], "float32"),
-    "vp": ("sbuf", [128, 2], "float32"),
+    "ap": ("sbuf", [128, 2], "float32"),
+    "qa": ("sbuf", [128, 2], "float32"),
+    "sa": ("sbuf", [128, 2], "float32"),
+    "m1": ("sbuf", [128, 2], "float32"),
+    "m0": ("sbuf", [128, 2], "float32"),
+    "h1": ("sbuf", [128, 2], "float32"),
+    "h0": ("sbuf", [128, 2], "float32"),
+    "t1": ("sbuf", [128, 2], "float32"),
+    "t2": ("sbuf", [128, 2], "float32"),
+    "t3": ("sbuf", [128, 2], "float32"),
+    "su": ("sbuf", [128, 2], "float32"),
     "z": ("sbuf", [128, 6], "float32"),
-    "w": ("sbuf", [128, 6], "float32"),
+    "w": ("sbuf", [128, 4], "float32"),
     "o": ("sbuf", [128, 6], "float32"),
     "ps_part": ("psum", [128, 512], "float32"),
     "ps_a": ("psum", [128, 512], "float32"),
     "ps_b": ("psum", [128, 512], "float32"),
 }
-SEMAPHORES = ["ld", "cst", "idn", "sq0", "sq1", "mm", "pr", "arr", "sent", "rd", "vq", "sr", "sc0", "sc1",
-              "dg0", "dg1", "bc0", "bc1", "ml0", "ml1", "st"]
+SEMAPHORES = ["ld", "cst", "idn", "sq0", "sq1", "mm", "pr", "arr", "sent", "ev", "sra", "rd0", "rd1", "s0", "s1",
+              "hu", "rc0", "rc1", "sc0", "sc1", "dg0", "dg1", "bc0", "bc1", "ml0", "ml1", "st"]
 
 
 def _engines(mask, n):
@@ -84,6 +95,7 @@ def rank_program(g, core, T, topo):
     plan = _plan(T, topo)
     rank = T.rank_of(core)
     mult, add = AluOpType.mult, AluOpType.add
+    Act = ActivationFunctionType
 
     if rank is None:
         for c in plan:
@@ -110,19 +122,22 @@ def rank_program(g, core, T, topo):
 
     sy.dma_start(T.xs[:], T.x[:]).then_inc(S.ld, 16)
     v.memset(T.ones[:], 1.0).then_inc(S.cst, 1)
-    v.memset(T.shm[:], SH).then_inc(S.cst, 1)
-    v.memset(T.w[:], 0.0).then_inc(S.cst, 1)
-    g.wait_ge(S.cst, 3)
+    v.memset(T.w[:, 3:4], 1.0 / D).then_inc(S.cst, 1)
+    v.memset(T.shm[:], C).then_inc(S.cst, 1)
+    v.memset(T.w[:, 0:1], 0.0).then_inc(S.cst, 1)
+    v.memset(T.w[:, 1:2], 1.5).then_inc(S.cst, 1)
+    v.memset(T.w[:, 2:3], 0.0).then_inc(S.cst, 1)
+    g.wait_ge(S.cst, 6)
     g.affine_select(T.ident[:], T.ones[:], [[-1, 128]], AluOpType.is_equal, 0.0, 0, 1).then_inc(S.idn, 1)
 
     a.wait_ge(S.ld, 16)
-    a.activation(T.sq[:, 0:HALF], T.xs[:, 0:HALF], ActivationFunctionType.Square, scale=SH).then_inc(S.sq0, 1)
-    a.activation(T.sq[:, HALF:TK], T.xs[:, HALF:TK], ActivationFunctionType.Square, scale=SH).then_inc(S.sq1, 1)
-    pe.wait_ge(S.cst, 3)
+    a.activation(T.sq[:, 0:HALF], T.xs[:, 0:HALF], Act.Square, scale=SH).then_inc(S.sq0, 1)
+    a.activation(T.sq[:, HALF:TK], T.xs[:, HALF:TK], Act.Square, scale=SH).then_inc(S.sq1, 1)
+    pe.wait_ge(S.cst, 6)
     pe.wait_ge(S.sq0, 1)
-    pe.matmul(T.ps_part[:, 0:1], T.sq[:, 0:HALF], T.ones[:, 0:1], True, True).then_inc(S.mm, 1)
+    pe.matmul(T.ps_part[:, 0:1], T.sq[:, 0:HALF], T.w[:, 3:4], True, True).then_inc(S.mm, 1)
     pe.wait_ge(S.sq1, 1)
-    pe.matmul(T.ps_part[:, 1:2], T.sq[:, HALF:TK], T.ones[:, 0:1], True, True).then_inc(S.mm, 1)
+    pe.matmul(T.ps_part[:, 1:2], T.sq[:, HALF:TK], T.w[:, 3:4], True, True).then_inc(S.mm, 1)
     v.wait_ge(S.mm, 2)
     v.tensor_copy(mine, T.ps_part[:, 0:2]).then_inc(S.pr, 1)
 
@@ -130,28 +145,51 @@ def rank_program(g, core, T, topo):
     _send(g, T, topo, core, [h for h, _s in relays], mine, E_RANK)
     _send(g, T, topo, core, direct, mine, E_RANK)
 
+    a.wait_ge(S.pr, 1)
+    a.activation(T.sa[:], mine, Act.Sqrt, bias=EPS * C, scale=1.0).then_inc(S.sra, 1)
     v.wait_ge(S.pr, 1)
-    v.wait_ge(S.arr, expected)
-    v.tensor_reduce(T.tot[:, 0:1], T.land[:, 0:SLOT * N:SLOT], AxisListType.X, add).then_inc(S.rd, 1)
-    v.tensor_reduce(T.tot[:, 1:2], T.land[:, 1:SLOT * N:SLOT], AxisListType.X, add).then_inc(S.rd, 1)
-    a.wait_ge(S.rd, 2)
-    a.activation(T.z[:, 1:6:3], T.tot[:], ActivationFunctionType.Sqrt, bias=EPS * C, scale=1.0 / D).then_inc(S.sr, 1)
-    v.wait_ge(S.rd, 2)
-    v.tensor_scalar(T.vp[:], T.tot[:], 1.0 / D, EPS * C, mult, add).then_inc(S.vq, 1)
-    v.wait_ge(S.vq, 1)
-    v.reciprocal(T.z[:, 0:6:3], T.vp[:]).then_inc(S.vq, 1)
-    v.wait_ge(S.vq, 2)
-    v.tensor_scalar(T.z[:, 2:6:3], T.z[:, 0:6:3], -0.5, None, mult).then_inc(S.vq, 1)
-    v.tensor_scalar(T.w[:, 2:6:3], T.z[:, 0:6:3], 1.5, None, mult).then_inc(S.vq, 1)
-    v.wait_ge(S.vq, 4)
-    v.wait_ge(S.cst, 3)
+    v.tensor_scalar(T.ap[:], mine, EPS * C, None, add).then_inc(S.ev, 1)
+    v.wait_ge(S.ev, 1)
+    v.reciprocal(T.qa[:], T.ap[:]).then_inc(S.ev, 1)
+    v.wait_ge(S.ev, 2)
+    v.tensor_scalar(T.m1[:], T.qa[:], K, None, mult).then_inc(S.ev, 1)
+    v.tensor_scalar(T.m0[:], T.qa[:], EPS * C * K, None, mult).then_inc(S.ev, 1)
+    v.tensor_scalar(T.h1[:], T.qa[:], -0.5 * K, None, mult).then_inc(S.ev, 1)
+    v.tensor_scalar(T.h0[:], T.qa[:], -0.5 * EPS * C * K, None, mult).then_inc(S.ev, 1)
+    v.wait_ge(S.sra, 1)
+    v.tensor_tensor(T.t1[:], T.sa[:], T.qa[:], mult).then_inc(S.ev, 1)
+    v.wait_ge(S.ev, 7)
+    v.tensor_tensor(T.t2[:], T.sa[:], T.t1[:], mult).then_inc(S.ev, 1)
+    v.wait_ge(S.ev, 8)
+    v.tensor_scalar(T.t3[:], T.t2[:], -0.5, 1.5, mult, add).then_inc(S.ev, 1)
+    v.wait_ge(S.ev, 9)
+    v.tensor_tensor(T.z[:, 2:6:3], T.t1[:], T.t3[:], mult).then_inc(S.ev, 1)
+    v.wait_ge(S.ev, 10)
+    v.wait_ge(S.cst, 6)
     v.wait_ge(S.idn, 1)
     v.wait_ge(S.ld, 16)
-    v.wait_ge(S.sr, 1)
+
+    v.wait_ge(S.arr, expected)
+    v.tensor_reduce(T.tot[:, 0:1], T.land[:, 0:SLOT * N:SLOT], AxisListType.X, add).then_inc(S.rd0, 1)
+    v.tensor_reduce(T.tot[:, 1:2], T.land[:, 1:SLOT * N:SLOT], AxisListType.X, add).then_inc(S.rd1, 1)
+    a.wait_ge(S.ev, 10)
+    a.wait_ge(S.rd0, 1)
+    a.activation(T.su[:, 0:1], T.tot[:, 0:1], Act.Sqrt, bias=T.m0[:, 0:1], scale=T.m1[:, 0:1]).then_inc(S.s0, 1)
+    a.wait_ge(S.rd1, 1)
+    a.activation(T.su[:, 1:2], T.tot[:, 1:2], Act.Sqrt, bias=T.m0[:, 1:2], scale=T.m1[:, 1:2]).then_inc(S.s1, 1)
+    a.activation(T.z[:, 0:1], T.tot[:, 0:1], Act.Identity, bias=T.h0[:, 0:1], scale=T.h1[:, 0:1]).then_inc(S.hu, 1)
+    a.activation(T.z[:, 3:4], T.tot[:, 1:2], Act.Identity, bias=T.h0[:, 1:2], scale=T.h1[:, 1:2]).then_inc(S.hu, 1)
+    v.wait_ge(S.s0, 1)
+    v.reciprocal(T.z[:, 1:2], T.su[:, 0:1]).then_inc(S.rc0, 1)
+    v.wait_ge(S.rc0, 1)
+    v.wait_ge(S.hu, 2)
     v.tensor_tensor_scan(T.o[:, 0:3], T.z[:, 0:3], T.w[:, 0:3], T.z[:, 1:2], mult, add).then_inc(S.sc0, 1)
     v.wait_ge(S.sc0, 1)
     v.tensor_scalar(T.diag[:, 0:HALF], T.ident[:], T.z[:, 1:2], T.o[:, 2:3], mult, mult).then_inc(S.dg0, 1)
-    v.tensor_tensor_scan(T.o[:, 3:6], T.z[:, 3:6], T.w[:, 3:6], T.z[:, 4:5], mult, add).then_inc(S.sc1, 1)
+    v.wait_ge(S.s1, 1)
+    v.reciprocal(T.z[:, 4:5], T.su[:, 1:2]).then_inc(S.rc1, 1)
+    v.wait_ge(S.rc1, 1)
+    v.tensor_tensor_scan(T.o[:, 3:6], T.z[:, 3:6], T.w[:, 0:3], T.z[:, 4:5], mult, add).then_inc(S.sc1, 1)
     v.wait_ge(S.sc1, 1)
     v.tensor_scalar(T.diag[:, HALF:TK], T.ident[:], T.z[:, 4:5], T.o[:, 5:6], mult, mult).then_inc(S.dg1, 1)
 

@@ -11,6 +11,7 @@ SH = 2.0 ** -22
 C = SH * SH
 K = 2.0 ** -44
 SLOT = 4
+NS = SLOT * (N + 1)
 
 NH = 2
 E_RANK = 8
@@ -24,28 +25,21 @@ SCRATCH = {
     "shm": ("sbuf", [128, 128], "float32"),
     "ident": ("sbuf", [128, 128], "float32"),
     "diag": ("sbuf", [128, TK], "float32"),
-    "land": ("sbuf", [128, SLOT * N], "float32"),
+    "land": ("sbuf", [128, NS], "float32"),
     "tot": ("sbuf", [128, 2], "float32"),
     "ap": ("sbuf", [128, 2], "float32"),
     "qa": ("sbuf", [128, 2], "float32"),
     "sa": ("sbuf", [128, 2], "float32"),
     "m1": ("sbuf", [128, 2], "float32"),
-    "m0": ("sbuf", [128, 2], "float32"),
-    "h1": ("sbuf", [128, 2], "float32"),
-    "h0": ("sbuf", [128, 2], "float32"),
-    "t1": ("sbuf", [128, 2], "float32"),
-    "t2": ("sbuf", [128, 2], "float32"),
-    "t3": ("sbuf", [128, 2], "float32"),
-    "su": ("sbuf", [128, 2], "float32"),
-    "z": ("sbuf", [128, 6], "float32"),
-    "w": ("sbuf", [128, 4], "float32"),
-    "o": ("sbuf", [128, 6], "float32"),
+    "z": ("sbuf", [128, 8], "float32"),
+    "w": ("sbuf", [128, 5], "float32"),
+    "o": ("sbuf", [128, 8], "float32"),
     "ps_part": ("psum", [128, 512], "float32"),
     "ps_a": ("psum", [128, 512], "float32"),
     "ps_b": ("psum", [128, 512], "float32"),
 }
-SEMAPHORES = ["ld", "cst", "idn", "sq0", "sq1", "mm", "pr", "arr", "sent", "ev", "sra", "rd0", "rd1", "s0", "s1",
-              "hu", "rc0", "rc1", "sc0", "sc1", "dg0", "dg1", "bc0", "bc1", "ml0", "ml1", "st"]
+SEMAPHORES = ["ld", "cst", "idn", "sq0", "sq1", "mm", "pr", "arr", "sent", "ev", "sra", "rd", "su", "rc", "sc",
+              "dg0", "dg1", "bc0", "bc1", "ml0", "ml1", "st"]
 
 
 def _engines(mask, n):
@@ -119,25 +113,26 @@ def rank_program(g, core, T, topo):
     mine = T.land[:, SLOT * rank:SLOT * rank + 2]
     v, a, pe, sy = g.vector, g.scalar, g.tensor, g.sync
     S = T.sem
+    NC = 6
 
     sy.dma_start(T.xs[:], T.x[:]).then_inc(S.ld, 16)
     v.memset(T.ones[:], 1.0).then_inc(S.cst, 1)
-    v.memset(T.w[:, 3:4], 1.0 / D).then_inc(S.cst, 1)
-    v.memset(T.shm[:], C).then_inc(S.cst, 1)
-    v.memset(T.w[:, 0:1], 0.0).then_inc(S.cst, 1)
-    v.memset(T.w[:, 1:2], 1.5).then_inc(S.cst, 1)
-    v.memset(T.w[:, 2:3], 0.0).then_inc(S.cst, 1)
-    g.wait_ge(S.cst, 6)
+    v.memset(T.w[:, 4:5], 1.0 / D).then_inc(S.cst, 1)
+    v.memset(T.shm[:], SH).then_inc(S.cst, 1)
+    v.memset(T.w[:, 0:3], 0.0).then_inc(S.cst, 1)
+    v.memset(T.w[:, 3:4], 1.5).then_inc(S.cst, 1)
+    v.memset(T.land[:, SLOT * N:SLOT * N + 2], EPS * C).then_inc(S.cst, 1)
+    g.wait_ge(S.cst, NC)
     g.affine_select(T.ident[:], T.ones[:], [[-1, 128]], AluOpType.is_equal, 0.0, 0, 1).then_inc(S.idn, 1)
 
     a.wait_ge(S.ld, 16)
     a.activation(T.sq[:, 0:HALF], T.xs[:, 0:HALF], Act.Square, scale=SH).then_inc(S.sq0, 1)
     a.activation(T.sq[:, HALF:TK], T.xs[:, HALF:TK], Act.Square, scale=SH).then_inc(S.sq1, 1)
-    pe.wait_ge(S.cst, 6)
+    pe.wait_ge(S.cst, NC)
     pe.wait_ge(S.sq0, 1)
-    pe.matmul(T.ps_part[:, 0:1], T.sq[:, 0:HALF], T.w[:, 3:4], True, True).then_inc(S.mm, 1)
+    pe.matmul(T.ps_part[:, 0:1], T.sq[:, 0:HALF], T.w[:, 4:5], True, True).then_inc(S.mm, 1)
     pe.wait_ge(S.sq1, 1)
-    pe.matmul(T.ps_part[:, 1:2], T.sq[:, HALF:TK], T.w[:, 3:4], True, True).then_inc(S.mm, 1)
+    pe.matmul(T.ps_part[:, 1:2], T.sq[:, HALF:TK], T.w[:, 4:5], True, True).then_inc(S.mm, 1)
     v.wait_ge(S.mm, 2)
     v.tensor_copy(mine, T.ps_part[:, 0:2]).then_inc(S.pr, 1)
 
@@ -153,46 +148,30 @@ def rank_program(g, core, T, topo):
     v.reciprocal(T.qa[:], T.ap[:]).then_inc(S.ev, 1)
     v.wait_ge(S.ev, 2)
     v.tensor_scalar(T.m1[:], T.qa[:], K, None, mult).then_inc(S.ev, 1)
-    v.tensor_scalar(T.m0[:], T.qa[:], EPS * C * K, None, mult).then_inc(S.ev, 1)
-    v.tensor_scalar(T.h1[:], T.qa[:], -0.5 * K, None, mult).then_inc(S.ev, 1)
-    v.tensor_scalar(T.h0[:], T.qa[:], -0.5 * EPS * C * K, None, mult).then_inc(S.ev, 1)
     v.wait_ge(S.sra, 1)
-    v.tensor_tensor(T.t1[:], T.sa[:], T.qa[:], mult).then_inc(S.ev, 1)
-    v.wait_ge(S.ev, 7)
-    v.tensor_tensor(T.t2[:], T.sa[:], T.t1[:], mult).then_inc(S.ev, 1)
-    v.wait_ge(S.ev, 8)
-    v.tensor_scalar(T.t3[:], T.t2[:], -0.5, 1.5, mult, add).then_inc(S.ev, 1)
-    v.wait_ge(S.ev, 9)
-    v.tensor_tensor(T.z[:, 2:6:3], T.t1[:], T.t3[:], mult).then_inc(S.ev, 1)
-    v.wait_ge(S.ev, 10)
-    v.wait_ge(S.cst, 6)
+    v.tensor_scalar(T.z[:, 0:8:4], T.sa[:], 1.0 / SH, None, mult).then_inc(S.ev, 1)
+    v.tensor_scalar(T.z[:, 3:8:4], T.sa[:], -0.5 / SH, None, mult).then_inc(S.ev, 1)
+    v.wait_ge(S.ev, 5)
+    v.wait_ge(S.cst, NC)
     v.wait_ge(S.idn, 1)
     v.wait_ge(S.ld, 16)
+    a.wait_ge(S.ev, 5)
 
     v.wait_ge(S.arr, expected)
-    v.tensor_reduce(T.tot[:, 0:1], T.land[:, 0:SLOT * N:SLOT], AxisListType.X, add).then_inc(S.rd0, 1)
-    v.tensor_reduce(T.tot[:, 1:2], T.land[:, 1:SLOT * N:SLOT], AxisListType.X, add).then_inc(S.rd1, 1)
-    a.wait_ge(S.ev, 10)
-    a.wait_ge(S.rd0, 1)
-    a.activation(T.su[:, 0:1], T.tot[:, 0:1], Act.Sqrt, bias=T.m0[:, 0:1], scale=T.m1[:, 0:1]).then_inc(S.s0, 1)
-    a.wait_ge(S.rd1, 1)
-    a.activation(T.su[:, 1:2], T.tot[:, 1:2], Act.Sqrt, bias=T.m0[:, 1:2], scale=T.m1[:, 1:2]).then_inc(S.s1, 1)
-    a.activation(T.z[:, 0:1], T.tot[:, 0:1], Act.Identity, bias=T.h0[:, 0:1], scale=T.h1[:, 0:1]).then_inc(S.hu, 1)
-    a.activation(T.z[:, 3:4], T.tot[:, 1:2], Act.Identity, bias=T.h0[:, 1:2], scale=T.h1[:, 1:2]).then_inc(S.hu, 1)
-    v.wait_ge(S.s0, 1)
-    v.reciprocal(T.z[:, 1:2], T.su[:, 0:1]).then_inc(S.rc0, 1)
-    v.wait_ge(S.rc0, 1)
-    v.wait_ge(S.hu, 2)
-    v.tensor_tensor_scan(T.o[:, 0:3], T.z[:, 0:3], T.w[:, 0:3], T.z[:, 1:2], mult, add).then_inc(S.sc0, 1)
-    v.wait_ge(S.sc0, 1)
-    v.tensor_scalar(T.diag[:, 0:HALF], T.ident[:], T.z[:, 1:2], T.o[:, 2:3], mult, mult).then_inc(S.dg0, 1)
-    v.wait_ge(S.s1, 1)
-    v.reciprocal(T.z[:, 4:5], T.su[:, 1:2]).then_inc(S.rc1, 1)
-    v.wait_ge(S.rc1, 1)
-    v.tensor_tensor_scan(T.o[:, 3:6], T.z[:, 3:6], T.w[:, 0:3], T.z[:, 4:5], mult, add).then_inc(S.sc1, 1)
-    v.wait_ge(S.sc1, 1)
-    v.tensor_scalar(T.diag[:, HALF:TK], T.ident[:], T.z[:, 4:5], T.o[:, 5:6], mult, mult).then_inc(S.dg1, 1)
-
+    v.tensor_reduce(T.tot[:, 0:1], T.land[:, 0:NS:SLOT], AxisListType.X, add).then_inc(S.rd, 1)
+    v.tensor_reduce(T.tot[:, 1:2], T.land[:, 1:NS:SLOT], AxisListType.X, add).then_inc(S.rd, 1)
+    a.wait_ge(S.rd, 2)
+    a.activation(T.z[:, 2:3], T.tot[:, 0:1], Act.Sqrt, scale=T.m1[:, 0:1]).then_inc(S.su, 1)
+    a.activation(T.z[:, 6:7], T.tot[:, 1:2], Act.Sqrt, scale=T.m1[:, 1:2]).then_inc(S.su, 1)
+    v.wait_ge(S.rd, 2)
+    v.reciprocal(T.z[:, 1:8:4], T.tot[:]).then_inc(S.rc, 1)
+    v.wait_ge(S.rc, 1)
+    v.wait_ge(S.su, 2)
+    v.tensor_tensor_scan(T.o[:, 0:4], T.z[:, 0:4], T.w[:, 0:4], T.z[:, 2:3], mult, add).then_inc(S.sc, 1)
+    v.tensor_tensor_scan(T.o[:, 4:8], T.z[:, 4:8], T.w[:, 0:4], T.z[:, 6:7], mult, add).then_inc(S.sc, 1)
+    v.wait_ge(S.sc, 2)
+    v.tensor_scalar(T.diag[:, 0:HALF], T.ident[:], T.o[:, 1:2], T.o[:, 3:4], mult, mult).then_inc(S.dg0, 1)
+    v.tensor_scalar(T.diag[:, HALF:TK], T.ident[:], T.o[:, 5:6], T.o[:, 7:8], mult, mult).then_inc(S.dg1, 1)
     pe.wait_ge(S.dg0, 1)
     pe.matmul(T.ps_a[:, 0:HALF], T.shm[:], T.diag[:, 0:HALF], True, True).then_inc(S.bc0, 1)
     pe.wait_ge(S.dg1, 1)

@@ -16,6 +16,7 @@ NS = SLOT * (N + 1)
 NH = 2
 E_RANK = 8
 E_RELAY = 8
+MATS = ["ident", "shm"]
 
 SCRATCH = {
     "xs": ("sbuf", [128, TK], "float32"),
@@ -38,7 +39,7 @@ SCRATCH = {
     "ps_a": ("psum", [128, 512], "float32"),
     "ps_b": ("psum", [128, 512], "float32"),
 }
-SEMAPHORES = ["ld", "cst", "idn", "sq0", "sq1", "mm", "pr", "arr", "sent", "ev", "sra", "rd", "su", "rc", "sc",
+SEMAPHORES = ["ld", "cst", "idn", "cin", "sq0", "sq1", "mm", "pr", "arr", "sent", "ev", "sra", "rd", "su", "rc", "sc",
               "dg0", "dg1", "bc0", "bc1", "ml0", "ml1", "st"]
 
 
@@ -74,14 +75,14 @@ def _plan(T, topo):
     return plan
 
 
-def _send(g, T, topo, src_core, dsts, ap, n_eng):
+def _send(g, T, topo, dsts, ap, mask, sem):
     ids = []
     for d in dsts:
         rid, pid, _se = topo.addr(d)
         ids.append(DstId(rid=rid, pnc=pid))
     g.remote_dma_fused(
-        [RemoteDMATransfer(dst_ids=ids, dma_engine_mask=_common_mask(topo, src_core, dsts, n_eng),
-                           remote_sem=T.sem.arr, srcs=[ap], dsts=[ap for _d in dsts], alu_op=0)],
+        [RemoteDMATransfer(dst_ids=ids, dma_engine_mask=mask,
+                           remote_sem=sem, srcs=[ap], dsts=[ap for _d in dsts], alu_op=0)],
         local_sem=T.sem.sent)
 
 
@@ -90,16 +91,33 @@ def rank_program(g, core, T, topo):
     rank = T.rank_of(core)
     mult, add = AluOpType.mult, AluOpType.add
     Act = ActivationFunctionType
+    S = T.sem
 
     if rank is None:
         for c in plan:
-            for h, share in plan[c][1]:
-                if h == core:
-                    r = T.rank_of(c)
-                    slot = T.land[:, SLOT * r:SLOT * r + 2]
-                    g.wait_ge(T.sem.arr, E_RANK)
-                    _send(g, T, topo, core, share, slot, E_RELAY)
-                    g.wait_ge(T.sem.sent, E_RELAY)
+            relays = plan[c][1]
+            for i, (h, share) in enumerate(relays):
+                if h != core:
+                    continue
+                mask = _common_mask(topo, core, [c] + share, E_RELAY)
+                calls = 0
+                for name in MATS[i::len(relays)]:
+                    if name == "ident":
+                        g.vector.memset(T.ones[:], 1.0).then_inc(S.cst, 1)
+                        g.wait_ge(S.cst, 1)
+                        g.affine_select(T.ident[:], T.ones[:], [[-1, 128]], AluOpType.is_equal, 0.0, 0, 1).then_inc(
+                            S.idn, 1)
+                        g.wait_ge(S.idn, 1)
+                    else:
+                        g.vector.memset(T.shm[:], SH).then_inc(S.ev, 1)
+                        g.wait_ge(S.ev, 1)
+                    _send(g, T, topo, [c], T[name][:], mask, S.cin)
+                    calls += 1
+                r = T.rank_of(c)
+                slot = T.land[:, SLOT * r:SLOT * r + 2]
+                g.wait_ge(S.arr, E_RANK)
+                _send(g, T, topo, share, slot, mask, S.arr)
+                g.wait_ge(S.sent, E_RELAY * (calls + 1))
         return
 
     direct, relays = plan[core]
@@ -112,18 +130,14 @@ def rank_program(g, core, T, topo):
                 expected += E_RELAY
     mine = T.land[:, SLOT * rank:SLOT * rank + 2]
     v, a, pe, sy = g.vector, g.scalar, g.tensor, g.sync
-    S = T.sem
-    NC = 6
+    NC = 4
+    CIN = E_RELAY * len(MATS)
 
     sy.dma_start(T.xs[:], T.x[:]).then_inc(S.ld, 16)
-    v.memset(T.ones[:], 1.0).then_inc(S.cst, 1)
     v.memset(T.w[:, 4:5], 1.0 / D).then_inc(S.cst, 1)
-    v.memset(T.shm[:], SH).then_inc(S.cst, 1)
     v.memset(T.w[:, 0:3], 0.0).then_inc(S.cst, 1)
     v.memset(T.w[:, 3:4], 1.5).then_inc(S.cst, 1)
     v.memset(T.land[:, SLOT * N:SLOT * N + 2], EPS * C).then_inc(S.cst, 1)
-    g.wait_ge(S.cst, NC)
-    g.affine_select(T.ident[:], T.ones[:], [[-1, 128]], AluOpType.is_equal, 0.0, 0, 1).then_inc(S.idn, 1)
 
     a.wait_ge(S.ld, 16)
     a.activation(T.sq[:, 0:HALF], T.xs[:, 0:HALF], Act.Square, scale=SH).then_inc(S.sq0, 1)
@@ -137,8 +151,9 @@ def rank_program(g, core, T, topo):
     v.tensor_copy(mine, T.ps_part[:, 0:2]).then_inc(S.pr, 1)
 
     g.wait_ge(S.pr, 1)
-    _send(g, T, topo, core, [h for h, _s in relays], mine, E_RANK)
-    _send(g, T, topo, core, direct, mine, E_RANK)
+    hs = [h for h, _s in relays]
+    _send(g, T, topo, hs, mine, _common_mask(topo, core, hs, E_RANK), S.arr)
+    _send(g, T, topo, direct, mine, _common_mask(topo, core, direct, E_RANK), S.arr)
 
     a.wait_ge(S.pr, 1)
     a.activation(T.sa[:], mine, Act.Sqrt, bias=EPS * C, scale=1.0).then_inc(S.sra, 1)
@@ -153,9 +168,10 @@ def rank_program(g, core, T, topo):
     v.tensor_scalar(T.z[:, 3:8:4], T.sa[:], -0.5 / SH, None, mult).then_inc(S.ev, 1)
     v.wait_ge(S.ev, 5)
     v.wait_ge(S.cst, NC)
-    v.wait_ge(S.idn, 1)
+    v.wait_ge(S.cin, CIN)
     v.wait_ge(S.ld, 16)
     a.wait_ge(S.ev, 5)
+    pe.wait_ge(S.cin, CIN)
 
     v.wait_ge(S.arr, expected)
     v.tensor_reduce(T.tot[:, 0:1], T.land[:, 0:NS:SLOT], AxisListType.X, add).then_inc(S.rd, 1)

@@ -11,9 +11,10 @@ SH = 2.0 ** -22
 C = SH * SH
 K = 2.0 ** -44
 SLOT = 4
-NS = SLOT * (N + 1)
+NS = SLOT * N
 
 NH = 2
+E_HAND = 16
 E_RANK = 8
 E_RELAY = 8
 MATS = ["ident", "shm"]
@@ -27,6 +28,7 @@ SCRATCH = {
     "ident": ("sbuf", [128, 128], "float32"),
     "diag": ("sbuf", [128, TK], "float32"),
     "land": ("sbuf", [128, NS], "float32"),
+    "epsc": ("sbuf", [128, 2], "float32"),
     "tot": ("sbuf", [128, 2], "float32"),
     "ap": ("sbuf", [128, 2], "float32"),
     "qa": ("sbuf", [128, 2], "float32"),
@@ -39,8 +41,8 @@ SCRATCH = {
     "ps_a": ("psum", [128, 512], "float32"),
     "ps_b": ("psum", [128, 512], "float32"),
 }
-SEMAPHORES = ["ld", "cst", "idn", "cin", "sq0", "sq1", "mm", "pr", "arr", "sent", "ev", "sra", "rd", "su", "rc", "sc",
-              "dg0", "dg1", "bc0", "bc1", "ml0", "ml1", "st"]
+SEMAPHORES = ["ld", "ec", "cst", "idn", "cin", "sq0", "sq1", "mm", "pr", "arr", "sent", "ev", "sra", "rd", "su", "rc",
+              "sc", "dg0", "dg1", "bc0", "bc1", "ml0", "ml1", "st"]
 
 
 def _engines(mask, n):
@@ -75,14 +77,14 @@ def _plan(T, topo):
     return plan
 
 
-def _send(g, T, topo, dsts, ap, mask, sem):
+def _send(g, T, topo, dsts, ap, mask, sem, src=None):
     ids = []
     for d in dsts:
         rid, pid, _se = topo.addr(d)
         ids.append(DstId(rid=rid, pnc=pid))
     g.remote_dma_fused(
         [RemoteDMATransfer(dst_ids=ids, dma_engine_mask=mask,
-                           remote_sem=sem, srcs=[ap], dsts=[ap for _d in dsts], alu_op=0)],
+                           remote_sem=sem, srcs=[ap if src is None else src], dsts=[ap for _d in dsts], alu_op=0)],
         local_sem=T.sem.sent)
 
 
@@ -114,8 +116,8 @@ def rank_program(g, core, T, topo):
                     _send(g, T, topo, [c], T[name][:], mask, S.cin)
                     calls += 1
                 r = T.rank_of(c)
-                slot = T.land[:, SLOT * r:SLOT * r + 2]
-                g.wait_ge(S.arr, E_RANK)
+                slot = T.land[:, SLOT * r:SLOT * r + SLOT]
+                g.wait_ge(S.arr, 2 * E_HAND)
                 _send(g, T, topo, share, slot, mask, S.arr)
                 g.wait_ge(S.sent, E_RELAY * (calls + 1))
         return
@@ -129,15 +131,23 @@ def rank_program(g, core, T, topo):
             if core in share:
                 expected += E_RELAY
     mine = T.land[:, SLOT * rank:SLOT * rank + 2]
+    mine_eps = T.land[:, SLOT * rank + 2:SLOT * rank + SLOT]
+    whole = T.land[:, SLOT * rank:SLOT * rank + SLOT]
     v, a, pe, sy = g.vector, g.scalar, g.tensor, g.sync
     NC = 4
     CIN = E_RELAY * len(MATS)
 
     sy.dma_start(T.xs[:], T.x[:]).then_inc(S.ld, 16)
+    v.memset(T.epsc[:], EPS * C / N).then_inc(S.ec, 1)
     v.memset(T.w[:, 4:5], 1.0 / D).then_inc(S.cst, 1)
     v.memset(T.w[:, 0:3], 0.0).then_inc(S.cst, 1)
     v.memset(T.w[:, 3:4], 1.5).then_inc(S.cst, 1)
-    v.memset(T.land[:, SLOT * N:SLOT * N + 2], EPS * C).then_inc(S.cst, 1)
+    v.memset(mine_eps, EPS * C / N).then_inc(S.cst, 1)
+
+    hs = [h for h, _s in relays]
+    hmask = _common_mask(topo, core, hs, E_HAND)
+    g.wait_ge(S.ec, 1)
+    _send(g, T, topo, hs, mine_eps, hmask, S.arr, src=T.epsc[:])
 
     a.wait_ge(S.ld, 16)
     a.activation(T.sq[:, 0:HALF], T.xs[:, 0:HALF], Act.Square, scale=SH).then_inc(S.sq0, 1)
@@ -150,10 +160,10 @@ def rank_program(g, core, T, topo):
     v.wait_ge(S.mm, 2)
     v.tensor_copy(mine, T.ps_part[:, 0:2]).then_inc(S.pr, 1)
 
+    g.wait_ge(S.cst, NC)
     g.wait_ge(S.pr, 1)
-    hs = [h for h, _s in relays]
-    _send(g, T, topo, hs, mine, _common_mask(topo, core, hs, E_RANK), S.arr)
-    _send(g, T, topo, direct, mine, _common_mask(topo, core, direct, E_RANK), S.arr)
+    _send(g, T, topo, hs, mine, hmask, S.arr)
+    _send(g, T, topo, direct, whole, _common_mask(topo, core, direct, E_RANK), S.arr)
 
     a.wait_ge(S.pr, 1)
     a.activation(T.sa[:], mine, Act.Sqrt, bias=EPS * C, scale=1.0).then_inc(S.sra, 1)
@@ -174,8 +184,8 @@ def rank_program(g, core, T, topo):
     pe.wait_ge(S.cin, CIN)
 
     v.wait_ge(S.arr, expected)
-    v.tensor_reduce(T.tot[:, 0:1], T.land[:, 0:NS:SLOT], AxisListType.X, add).then_inc(S.rd, 1)
-    v.tensor_reduce(T.tot[:, 1:2], T.land[:, 1:NS:SLOT], AxisListType.X, add).then_inc(S.rd, 1)
+    v.tensor_reduce(T.tot[:, 0:1], T.land[:, 0:NS:2], AxisListType.X, add).then_inc(S.rd, 1)
+    v.tensor_reduce(T.tot[:, 1:2], T.land[:, 1:NS:2], AxisListType.X, add).then_inc(S.rd, 1)
     a.wait_ge(S.rd, 2)
     a.activation(T.z[:, 2:3], T.tot[:, 0:1], Act.Sqrt, scale=T.m1[:, 0:1]).then_inc(S.su, 1)
     a.activation(T.z[:, 6:7], T.tot[:, 1:2], Act.Sqrt, scale=T.m1[:, 1:2]).then_inc(S.su, 1)
@@ -201,5 +211,5 @@ def rank_program(g, core, T, topo):
     a.wait_ge(S.ml1, 1)
     a.dma_start(T.y[:, HALF:TK], T.ys[:, HALF:TK]).then_inc(S.st, 16)
 
-    g.wait_ge(S.sent, 2 * E_RANK)
+    g.wait_ge(S.sent, 2 * E_HAND + E_RANK)
     sy.wait_ge(S.st, 32)

@@ -4,6 +4,7 @@ from concourse.mybir import AluOpType, AxisListType, ActivationFunctionType
 N = 6
 TK = 256
 HALF = 128
+BL = 64
 D = 128 * N
 EPS = 0.01
 SIM_CORES = 112
@@ -12,37 +13,45 @@ C = SH * SH
 K = 2.0 ** -44
 SLOT = 4
 NS = SLOT * N
+NA = NS // 2 + 1
+NP = 3 + HALF
 
 NH = 2
 E_HAND = 16
 E_RANK = 8
 E_RELAY = 8
-MATS = ["ident", "shm"]
 
 SCRATCH = {
     "xs": ("sbuf", [128, TK], "float32"),
     "sq": ("sbuf", [128, TK], "float32"),
     "ys": ("sbuf", [128, TK], "float32"),
     "ones": ("sbuf", [128, 128], "float32"),
-    "shm": ("sbuf", [128, 128], "float32"),
     "ident": ("sbuf", [128, 128], "float32"),
-    "diag": ("sbuf", [128, TK], "float32"),
-    "land": ("sbuf", [128, NS], "float32"),
+    "ida": ("sbuf", [128, TK], "float32"),
+    "rm": ("sbuf", [128, TK], "float32"),
+    "lb0": ("sbuf", [128, NP + 1], "float32"),
+    "lb1": ("sbuf", [128, NP + 1], "float32"),
+    "zz": ("sbuf", [128, 2 * NP + 2], "float32"),
+    "w1": ("sbuf", [128, NP + 1], "float32"),
+    "on": ("sbuf", [128, NA], "float32"),
+    "ss": ("sbuf", [128, 2 * NA], "float32"),
+    "land": ("sbuf", [128, NS + SLOT], "float32"),
     "epsc": ("sbuf", [128, 2], "float32"),
-    "tot": ("sbuf", [128, 2], "float32"),
+    "wc": ("sbuf", [128, 1], "float32"),
     "ap": ("sbuf", [128, 2], "float32"),
     "qa": ("sbuf", [128, 2], "float32"),
     "sa": ("sbuf", [128, 2], "float32"),
     "m1": ("sbuf", [128, 2], "float32"),
-    "z": ("sbuf", [128, 8], "float32"),
-    "w": ("sbuf", [128, 5], "float32"),
-    "o": ("sbuf", [128, 8], "float32"),
-    "ps_part": ("psum", [128, 512], "float32"),
-    "ps_a": ("psum", [128, 512], "float32"),
-    "ps_b": ("psum", [128, 512], "float32"),
+    "ps_pa": ("psum", [128, 512], "float32"),
+    "ps_pb": ("psum", [128, 512], "float32"),
+    "ps0": ("psum", [128, 512], "float32"),
+    "ps1": ("psum", [128, 512], "float32"),
+    "ps2": ("psum", [128, 512], "float32"),
+    "ps3": ("psum", [128, 512], "float32"),
 }
-SEMAPHORES = ["ld", "ec", "cst", "idn", "cin", "sq0", "sq1", "mm", "pr", "arr", "sent", "ev", "sra", "rd", "su", "rc",
-              "sc", "dg0", "dg1", "bc0", "bc1", "ml0", "ml1", "st"]
+SEMAPHORES = ["ld0", "ld1", "ec", "cst", "idn", "cin", "sq0", "sq1", "mm0", "mm1", "pr0", "pr", "arr", "sent", "ev",
+              "sra", "rd", "su0", "su1", "rc", "r0", "r1", "l0", "l1", "bc0", "bc1", "bc2", "bc3",
+              "ml0", "ml1", "ml2", "ml3", "st"]
 
 
 def _engines(mask, n):
@@ -102,24 +111,19 @@ def rank_program(g, core, T, topo):
                 if h != core:
                     continue
                 mask = _common_mask(topo, core, [c] + share, E_RELAY)
-                calls = 0
-                for name in MATS[i::len(relays)]:
-                    if name == "ident":
-                        g.vector.memset(T.ones[:], 1.0).then_inc(S.cst, 1)
-                        g.wait_ge(S.cst, 1)
-                        g.affine_select(T.ident[:], T.ones[:], [[-1, 128]], AluOpType.is_equal, 0.0, 0, 1).then_inc(
-                            S.idn, 1)
-                        g.wait_ge(S.idn, 1)
-                    else:
-                        g.vector.memset(T.shm[:], SH).then_inc(S.ev, 1)
-                        g.wait_ge(S.ev, 1)
-                    _send(g, T, topo, [c], T[name][:], mask, S.cin)
-                    calls += 1
+                wd = 128 // len(relays)
+                lo = i * wd
+                g.vector.memset(T.ones[:, lo:lo + wd], 1.0).then_inc(S.cst, 1)
+                g.wait_ge(S.cst, 1)
+                g.affine_select(T.ident[:, lo:lo + wd], T.ones[:, lo:lo + wd], [[-1, wd]], AluOpType.is_equal, 0.0,
+                                -lo, 1).then_inc(S.idn, 1)
+                g.wait_ge(S.idn, 1)
+                _send(g, T, topo, [c], T.ident[:, lo:lo + wd], mask, S.cin)
                 r = T.rank_of(c)
                 slot = T.land[:, SLOT * r:SLOT * r + SLOT]
                 g.wait_ge(S.arr, 2 * E_HAND)
                 _send(g, T, topo, share, slot, mask, S.arr)
-                g.wait_ge(S.sent, E_RELAY * (calls + 1))
+                g.wait_ge(S.sent, E_RELAY * 2)
         return
 
     direct, relays = plan[core]
@@ -130,86 +134,118 @@ def rank_program(g, core, T, topo):
         for _h, share in plan[c][1]:
             if core in share:
                 expected += E_RELAY
-    mine = T.land[:, SLOT * rank:SLOT * rank + 2]
-    mine_eps = T.land[:, SLOT * rank + 2:SLOT * rank + SLOT]
-    whole = T.land[:, SLOT * rank:SLOT * rank + SLOT]
+    b0 = SLOT * rank
+    mine = T.land[:, b0:b0 + 2]
+    mine_eps = T.land[:, b0 + 2:b0 + SLOT]
+    whole = T.land[:, b0:b0 + SLOT]
     v, a, pe, sy = g.vector, g.scalar, g.tensor, g.sync
-    NC = 4
-    CIN = E_RELAY * len(MATS)
+    CIN = E_RELAY * len(relays)
 
-    sy.dma_start(T.xs[:], T.x[:]).then_inc(S.ld, 16)
+    sy.dma_start(T.xs[:, 0:HALF], T.x[:, 0:HALF]).then_inc(S.ld0, 16)
+    a.dma_start(T.xs[:, HALF:TK], T.x[:, HALF:TK]).then_inc(S.ld1, 16)
     v.memset(T.epsc[:], EPS * C / N).then_inc(S.ec, 1)
-    v.memset(T.w[:, 4:5], 1.0 / D).then_inc(S.cst, 1)
-    v.memset(T.w[:, 0:3], 0.0).then_inc(S.cst, 1)
-    v.memset(T.w[:, 3:4], 1.5).then_inc(S.cst, 1)
+    v.memset(T.wc[:], 1.0 / D).then_inc(S.cst, 1)
     v.memset(mine_eps, EPS * C / N).then_inc(S.cst, 1)
+    v.memset(T.land[:, NS:NS + SLOT], 0.0).then_inc(S.cst, 1)
+    v.memset(T.on[:], 1.0).then_inc(S.cst, 1)
+    v.memset(T.w1[:, 0:2], 0.0).then_inc(S.cst, 1)
+    v.memset(T.w1[:, 2:3], 1.5).then_inc(S.cst, 1)
+    v.memset(T.w1[:, 3:NP], 0.0).then_inc(S.cst, 1)
+    v.memset(T.zz[:, 8:2 * NP], 1.0).then_inc(S.cst, 1)
+    NC = 8
 
     hs = [h for h, _s in relays]
     hmask = _common_mask(topo, core, hs, E_HAND)
     g.wait_ge(S.ec, 1)
     _send(g, T, topo, hs, mine_eps, hmask, S.arr, src=T.epsc[:])
 
-    a.wait_ge(S.ld, 16)
+    a.wait_ge(S.ld0, 16)
     a.activation(T.sq[:, 0:HALF], T.xs[:, 0:HALF], Act.Square, scale=SH).then_inc(S.sq0, 1)
+    a.wait_ge(S.ld1, 16)
     a.activation(T.sq[:, HALF:TK], T.xs[:, HALF:TK], Act.Square, scale=SH).then_inc(S.sq1, 1)
     pe.wait_ge(S.cst, NC)
     pe.wait_ge(S.sq0, 1)
-    pe.matmul(T.ps_part[:, 0:1], T.sq[:, 0:HALF], T.w[:, 4:5], True, True).then_inc(S.mm, 1)
+    pe.matmul(T.ps_pa[:, 0:1], T.sq[:, 0:HALF], T.wc[:], True, True).then_inc(S.mm0, 1)
     pe.wait_ge(S.sq1, 1)
-    pe.matmul(T.ps_part[:, 1:2], T.sq[:, HALF:TK], T.w[:, 4:5], True, True).then_inc(S.mm, 1)
-    v.wait_ge(S.mm, 2)
-    v.tensor_copy(mine, T.ps_part[:, 0:2]).then_inc(S.pr, 1)
+    pe.matmul(T.ps_pb[:, 0:1], T.sq[:, HALF:TK], T.wc[:], True, True).then_inc(S.mm1, 1)
+    v.wait_ge(S.mm0, 1)
+    v.tensor_copy(T.land[:, b0:b0 + 1], T.ps_pa[:, 0:1]).then_inc(S.pr0, 1)
+    v.wait_ge(S.mm1, 1)
+    v.tensor_copy(T.land[:, b0 + 1:b0 + 2], T.ps_pb[:, 0:1]).then_inc(S.pr, 1)
 
     g.wait_ge(S.cst, NC)
+    g.wait_ge(S.pr0, 1)
     g.wait_ge(S.pr, 1)
     _send(g, T, topo, hs, mine, hmask, S.arr)
     _send(g, T, topo, direct, whole, _common_mask(topo, core, direct, E_RANK), S.arr)
 
+    a.wait_ge(S.pr0, 1)
+    a.activation(T.sa[:, 0:1], T.land[:, b0:b0 + 1], Act.Sqrt, bias=EPS * C, scale=1.0).then_inc(S.sra, 1)
     a.wait_ge(S.pr, 1)
-    a.activation(T.sa[:], mine, Act.Sqrt, bias=EPS * C, scale=1.0).then_inc(S.sra, 1)
+    a.activation(T.sa[:, 1:2], T.land[:, b0 + 1:b0 + 2], Act.Sqrt, bias=EPS * C, scale=1.0).then_inc(S.sra, 1)
+    v.wait_ge(S.pr0, 1)
     v.wait_ge(S.pr, 1)
     v.tensor_scalar(T.ap[:], mine, EPS * C, None, add).then_inc(S.ev, 1)
     v.wait_ge(S.ev, 1)
     v.reciprocal(T.qa[:], T.ap[:]).then_inc(S.ev, 1)
     v.wait_ge(S.ev, 2)
     v.tensor_scalar(T.m1[:], T.qa[:], K, None, mult).then_inc(S.ev, 1)
-    v.wait_ge(S.sra, 1)
-    v.tensor_scalar(T.z[:, 0:8:4], T.sa[:], 1.0 / SH, None, mult).then_inc(S.ev, 1)
-    v.tensor_scalar(T.z[:, 3:8:4], T.sa[:], -0.5 / SH, None, mult).then_inc(S.ev, 1)
-    v.wait_ge(S.ev, 5)
-    v.wait_ge(S.cst, NC)
+    v.wait_ge(S.sra, 2)
     v.wait_ge(S.cin, CIN)
-    v.wait_ge(S.ld, 16)
-    a.wait_ge(S.ev, 5)
-    pe.wait_ge(S.cin, CIN)
+    for h in range(2):
+        v.tensor_scalar(T.zz[:, 2 + h:3 + h], T.sa[:, h:h + 1], T.sa[:, h:h + 1], -0.5 / C, mult, mult).then_inc(
+            S.ev, 1)
+    for h in range(2):
+        v.tensor_scalar(T.ida[:, HALF * h:HALF * h + HALF], T.ident[:], T.sa[:, h:h + 1], None, mult).then_inc(
+            S.ev, 1)
+    NEV = 7
+    v.wait_ge(S.ev, NEV)
+    v.wait_ge(S.cst, NC)
+    v.wait_ge(S.ld0, 16)
+    v.wait_ge(S.ld1, 16)
+    a.wait_ge(S.ev, NEV)
 
     v.wait_ge(S.arr, expected)
-    v.tensor_reduce(T.tot[:, 0:1], T.land[:, 0:NS:2], AxisListType.X, add).then_inc(S.rd, 1)
-    v.tensor_reduce(T.tot[:, 1:2], T.land[:, 1:NS:2], AxisListType.X, add).then_inc(S.rd, 1)
+    for h in range(2):
+        v.tensor_tensor_scan(T.ss[:, h:2 * NA:2], T.on[:], T.land[:, h:2 * NA:2], 0.0, mult, add).then_inc(S.rd, 1)
+    e = 2 * NA - 4
     a.wait_ge(S.rd, 2)
-    a.activation(T.z[:, 2:3], T.tot[:, 0:1], Act.Sqrt, scale=T.m1[:, 0:1]).then_inc(S.su, 1)
-    a.activation(T.z[:, 6:7], T.tot[:, 1:2], Act.Sqrt, scale=T.m1[:, 1:2]).then_inc(S.su, 1)
+    a.activation(T.zz[:, 0:1], T.ss[:, e:e + 1], Act.Sqrt, scale=T.m1[:, 0:1]).then_inc(S.su0, 1)
+    a.activation(T.zz[:, 1:2], T.ss[:, e + 1:e + 2], Act.Sqrt, scale=T.m1[:, 1:2]).then_inc(S.su1, 1)
     v.wait_ge(S.rd, 2)
-    v.reciprocal(T.z[:, 1:8:4], T.tot[:]).then_inc(S.rc, 1)
+    v.reciprocal(T.zz[:, 4:8], T.ss[:, e:e + 4]).then_inc(S.rc, 1)
+    a.wait_ge(S.su0, 1)
+    a.activation(T.rm[:, 0:HALF], T.ida[:, 0:HALF], Act.Identity, scale=T.zz[:, 0:1]).then_inc(S.r0, 1)
+    a.wait_ge(S.su1, 1)
+    a.activation(T.rm[:, HALF:TK], T.ida[:, HALF:TK], Act.Identity, scale=T.zz[:, 1:2]).then_inc(S.r1, 1)
     v.wait_ge(S.rc, 1)
-    v.wait_ge(S.su, 2)
-    v.tensor_tensor_scan(T.o[:, 0:4], T.z[:, 0:4], T.w[:, 0:4], T.z[:, 2:3], mult, add).then_inc(S.sc, 1)
-    v.tensor_tensor_scan(T.o[:, 4:8], T.z[:, 4:8], T.w[:, 0:4], T.z[:, 6:7], mult, add).then_inc(S.sc, 1)
-    v.wait_ge(S.sc, 2)
-    v.tensor_scalar(T.diag[:, 0:HALF], T.ident[:], T.o[:, 1:2], T.o[:, 3:4], mult, mult).then_inc(S.dg0, 1)
-    v.tensor_scalar(T.diag[:, HALF:TK], T.ident[:], T.o[:, 5:6], T.o[:, 7:8], mult, mult).then_inc(S.dg1, 1)
-    pe.wait_ge(S.dg0, 1)
-    pe.matmul(T.ps_a[:, 0:HALF], T.shm[:], T.diag[:, 0:HALF], True, True).then_inc(S.bc0, 1)
-    pe.wait_ge(S.dg1, 1)
-    pe.matmul(T.ps_b[:, 0:HALF], T.shm[:], T.diag[:, HALF:TK], True, True).then_inc(S.bc1, 1)
-    v.wait_ge(S.bc0, 1)
-    v.tensor_tensor(T.ys[:, 0:HALF], T.xs[:, 0:HALF], T.ps_a[:, 0:HALF], mult).then_inc(S.ml0, 1)
-    v.wait_ge(S.bc1, 1)
-    v.tensor_tensor(T.ys[:, HALF:TK], T.xs[:, HALF:TK], T.ps_b[:, 0:HALF], mult).then_inc(S.ml1, 1)
+    v.wait_ge(S.su0, 1)
+    v.tensor_tensor_scan(T.lb0[:, 1:NP + 1], T.zz[:, 0:2 * NP:2], T.w1[:, 0:NP], T.zz[:, 0:1], mult, add).then_inc(
+        S.l0, 1)
+    v.wait_ge(S.su1, 1)
+    v.tensor_tensor_scan(T.lb1[:, 1:NP + 1], T.zz[:, 1:2 * NP:2], T.w1[:, 0:NP], T.zz[:, 1:2], mult, add).then_inc(
+        S.l1, 1)
+    for b in range(4):
+        if b == 0:
+            pe.wait_ge(S.l0, 1)
+            pe.wait_ge(S.r0, 1)
+        if b == 2:
+            pe.wait_ge(S.l1, 1)
+            pe.wait_ge(S.r1, 1)
+        lb = T.lb0 if b < 2 else T.lb1
+        pe.matmul(T["ps%d" % b][:, 0:BL], lb[:, 4:4 + HALF], T.rm[:, BL * b:BL * b + BL], True, True).then_inc(
+            S["bc%d" % b], 1)
+    for b in range(4):
+        v.wait_ge(S["bc%d" % b], 1)
+        v.tensor_tensor(T.ys[:, BL * b:BL * b + BL], T.xs[:, BL * b:BL * b + BL], T["ps%d" % b][:, 0:BL],
+                        mult).then_inc(S["ml%d" % b], 1)
     sy.wait_ge(S.ml0, 1)
+    sy.wait_ge(S.ml1, 1)
     sy.dma_start(T.y[:, 0:HALF], T.ys[:, 0:HALF]).then_inc(S.st, 16)
-    a.wait_ge(S.ml1, 1)
-    a.dma_start(T.y[:, HALF:TK], T.ys[:, HALF:TK]).then_inc(S.st, 16)
+    a.wait_ge(S.ml2, 1)
+    a.dma_start(T.y[:, HALF:HALF + BL], T.ys[:, HALF:HALF + BL]).then_inc(S.st, 16)
+    sy.wait_ge(S.ml3, 1)
+    sy.dma_start(T.y[:, HALF + BL:TK], T.ys[:, HALF + BL:TK]).then_inc(S.st, 16)
 
     g.wait_ge(S.sent, 2 * E_HAND + E_RANK)
-    sy.wait_ge(S.st, 32)
+    sy.wait_ge(S.st, 48)

from concourse.bass import DstId, RemoteDMATransfer
from concourse.mybir import AluOpType, AxisListType, ActivationFunctionType

N = 6
TK = 256
HALF = 128
BL = 64
D = 128 * N
EPS = 0.01
SIM_CORES = 112
SH = 2.0 ** -22
C = SH * SH
K = 2.0 ** -44
SLOT = 4
NS = SLOT * N
NA = NS // 2 + 1
NP = 3 + HALF

NH = 2
E_HAND = 16
E_RANK = 8
E_RELAY = 8

SCRATCH = {
    "xs": ("sbuf", [128, TK], "float32"),
    "sq": ("sbuf", [128, TK], "float32"),
    "ys": ("sbuf", [128, TK], "float32"),
    "ones": ("sbuf", [128, 128], "float32"),
    "ident": ("sbuf", [128, 128], "float32"),
    "ida": ("sbuf", [128, TK], "float32"),
    "rm": ("sbuf", [128, TK], "float32"),
    "lb0": ("sbuf", [128, NP + 1], "float32"),
    "lb1": ("sbuf", [128, NP + 1], "float32"),
    "zz": ("sbuf", [128, 2 * NP + 2], "float32"),
    "w1": ("sbuf", [128, NP + 1], "float32"),
    "on": ("sbuf", [128, NA], "float32"),
    "ss": ("sbuf", [128, 2 * NA], "float32"),
    "land": ("sbuf", [128, NS + SLOT], "float32"),
    "epsc": ("sbuf", [128, 2], "float32"),
    "wc": ("sbuf", [128, 1], "float32"),
    "ap": ("sbuf", [128, 2], "float32"),
    "qa": ("sbuf", [128, 2], "float32"),
    "sa": ("sbuf", [128, 2], "float32"),
    "m1": ("sbuf", [128, 2], "float32"),
    "ps_pa": ("psum", [128, 512], "float32"),
    "ps_pb": ("psum", [128, 512], "float32"),
    "ps0": ("psum", [128, 512], "float32"),
    "ps1": ("psum", [128, 512], "float32"),
    "ps2": ("psum", [128, 512], "float32"),
    "ps3": ("psum", [128, 512], "float32"),
}
SEMAPHORES = ["ld0", "ld1", "ec", "cst", "idn", "cin", "sq0", "sq1", "mm0", "mm1", "pr0", "pr", "arr", "sent", "ev",
              "sra", "rd", "su0", "su1", "rc", "r0", "r1", "l0", "l1", "bc0", "bc1", "bc2", "bc3",
              "ml0", "ml1", "ml2", "ml3", "st"]


def _engines(mask, n):
    out, bit, k = 0, 1, 0
    while k < n:
        if mask & bit:
            out |= bit
            k += 1
        bit <<= 1
    return out


def _common_mask(topo, src, dsts, n):
    m = topo.mask(src, dsts[0])
    for d in dsts[1:]:
        m &= topo.mask(src, d)
    return _engines(m, n)


def _plan(T, topo):
    group = list(T.cores)
    plan = {}
    for c in group:
        direct = [d for d in group if d != c and topo.may_write(c, d)]
        far = [d for d in group if d != c and not topo.may_write(c, d)]
        cand = [h for h in range(SIM_CORES)
                if topo.chip(h) == topo.chip(c) and h not in group and all(topo.may_write(h, d) for d in far)]
        cand.sort(key=lambda h: (topo.die(h) != topo.die(c), h))
        nh = min(NH, len(far), len(cand))
        relays = [(cand[i], far[i::nh]) for i in range(nh)]
        plan[c] = (direct, relays)
    return plan


def _send(g, T, topo, dsts, ap, mask, sem, src=None):
    ids = []
    for d in dsts:
        rid, pid, _se = topo.addr(d)
        ids.append(DstId(rid=rid, pnc=pid))
    g.remote_dma_fused(
        [RemoteDMATransfer(dst_ids=ids, dma_engine_mask=mask,
                           remote_sem=sem, srcs=[ap if src is None else src], dsts=[ap for _d in dsts], alu_op=0)],
        local_sem=T.sem.sent)


def rank_program(g, core, T, topo):
    plan = _plan(T, topo)
    rank = T.rank_of(core)
    mult, add = AluOpType.mult, AluOpType.add
    Act = ActivationFunctionType
    S = T.sem

    if rank is None:
        for c in plan:
            relays = plan[c][1]
            for i, (h, share) in enumerate(relays):
                if h != core:
                    continue
                mask = _common_mask(topo, core, [c] + share, E_RELAY)
                wd = 128 // len(relays)
                lo = i * wd
                g.vector.memset(T.ones[:, lo:lo + wd], 1.0).then_inc(S.cst, 1)
                g.wait_ge(S.cst, 1)
                g.affine_select(T.ident[:, lo:lo + wd], T.ones[:, lo:lo + wd], [[-1, wd]], AluOpType.is_equal, 0.0,
                                -lo, 1).then_inc(S.idn, 1)
                g.wait_ge(S.idn, 1)
                _send(g, T, topo, [c], T.ident[:, lo:lo + wd], mask, S.cin)
                r = T.rank_of(c)
                slot = T.land[:, SLOT * r:SLOT * r + SLOT]
                g.wait_ge(S.arr, 2 * E_HAND)
                _send(g, T, topo, share, slot, mask, S.arr)
                g.wait_ge(S.sent, E_RELAY * 2)
        return

    direct, relays = plan[core]
    expected = 0
    for c in plan:
        if core in plan[c][0]:
            expected += E_RANK
        for _h, share in plan[c][1]:
            if core in share:
                expected += E_RELAY
    b0 = SLOT * rank
    mine = T.land[:, b0:b0 + 2]
    mine_eps = T.land[:, b0 + 2:b0 + SLOT]
    whole = T.land[:, b0:b0 + SLOT]
    v, a, pe, sy = g.vector, g.scalar, g.tensor, g.sync
    CIN = E_RELAY * len(relays)

    sy.dma_start(T.xs[:, 0:HALF], T.x[:, 0:HALF]).then_inc(S.ld0, 16)
    a.dma_start(T.xs[:, HALF:TK], T.x[:, HALF:TK]).then_inc(S.ld1, 16)
    v.memset(T.epsc[:], EPS * C / N).then_inc(S.ec, 1)
    v.memset(T.wc[:], 1.0 / D).then_inc(S.cst, 1)
    v.memset(mine_eps, EPS * C / N).then_inc(S.cst, 1)
    v.memset(T.land[:, NS:NS + SLOT], 0.0).then_inc(S.cst, 1)
    v.memset(T.on[:], 1.0).then_inc(S.cst, 1)
    v.memset(T.w1[:, 0:2], 0.0).then_inc(S.cst, 1)
    v.memset(T.w1[:, 2:3], 1.5).then_inc(S.cst, 1)
    v.memset(T.w1[:, 3:NP], 0.0).then_inc(S.cst, 1)
    v.memset(T.zz[:, 8:2 * NP], 1.0).then_inc(S.cst, 1)
    NC = 8

    hs = [h for h, _s in relays]
    hmask = _common_mask(topo, core, hs, E_HAND)
    g.wait_ge(S.ec, 1)
    _send(g, T, topo, hs, mine_eps, hmask, S.arr, src=T.epsc[:])

    a.wait_ge(S.ld0, 16)
    a.activation(T.sq[:, 0:HALF], T.xs[:, 0:HALF], Act.Square, scale=SH).then_inc(S.sq0, 1)
    a.wait_ge(S.ld1, 16)
    a.activation(T.sq[:, HALF:TK], T.xs[:, HALF:TK], Act.Square, scale=SH).then_inc(S.sq1, 1)
    pe.wait_ge(S.cst, NC)
    pe.wait_ge(S.sq0, 1)
    pe.matmul(T.ps_pa[:, 0:1], T.sq[:, 0:HALF], T.wc[:], True, True).then_inc(S.mm0, 1)
    pe.wait_ge(S.sq1, 1)
    pe.matmul(T.ps_pb[:, 0:1], T.sq[:, HALF:TK], T.wc[:], True, True).then_inc(S.mm1, 1)
    v.wait_ge(S.mm0, 1)
    v.tensor_copy(T.land[:, b0:b0 + 1], T.ps_pa[:, 0:1]).then_inc(S.pr0, 1)
    v.wait_ge(S.mm1, 1)
    v.tensor_copy(T.land[:, b0 + 1:b0 + 2], T.ps_pb[:, 0:1]).then_inc(S.pr, 1)

    g.wait_ge(S.cst, NC)
    g.wait_ge(S.pr0, 1)
    g.wait_ge(S.pr, 1)
    _send(g, T, topo, hs, mine, hmask, S.arr)
    _send(g, T, topo, direct, whole, _common_mask(topo, core, direct, E_RANK), S.arr)

    a.wait_ge(S.pr0, 1)
    a.activation(T.sa[:, 0:1], T.land[:, b0:b0 + 1], Act.Sqrt, bias=EPS * C, scale=1.0).then_inc(S.sra, 1)
    a.wait_ge(S.pr, 1)
    a.activation(T.sa[:, 1:2], T.land[:, b0 + 1:b0 + 2], Act.Sqrt, bias=EPS * C, scale=1.0).then_inc(S.sra, 1)
    v.wait_ge(S.pr0, 1)
    v.wait_ge(S.pr, 1)
    v.tensor_scalar(T.ap[:], mine, EPS * C, None, add).then_inc(S.ev, 1)
    v.wait_ge(S.ev, 1)
    v.reciprocal(T.qa[:], T.ap[:]).then_inc(S.ev, 1)
    v.wait_ge(S.ev, 2)
    v.tensor_scalar(T.m1[:], T.qa[:], K, None, mult).then_inc(S.ev, 1)
    v.wait_ge(S.sra, 2)
    v.wait_ge(S.cin, CIN)
    for h in range(2):
        v.tensor_scalar(T.zz[:, 2 + h:3 + h], T.sa[:, h:h + 1], T.sa[:, h:h + 1], -0.5 / C, mult, mult).then_inc(
            S.ev, 1)
    for h in range(2):
        v.tensor_scalar(T.ida[:, HALF * h:HALF * h + HALF], T.ident[:], T.sa[:, h:h + 1], None, mult).then_inc(
            S.ev, 1)
    NEV = 7
    v.wait_ge(S.ev, NEV)
    v.wait_ge(S.cst, NC)
    v.wait_ge(S.ld0, 16)
    v.wait_ge(S.ld1, 16)
    a.wait_ge(S.ev, NEV)

    v.wait_ge(S.arr, expected)
    for h in range(2):
        v.tensor_tensor_scan(T.ss[:, h:2 * NA:2], T.on[:], T.land[:, h:2 * NA:2], 0.0, mult, add).then_inc(S.rd, 1)
    e = 2 * NA - 4
    a.wait_ge(S.rd, 2)
    a.activation(T.zz[:, 0:1], T.ss[:, e:e + 1], Act.Sqrt, scale=T.m1[:, 0:1]).then_inc(S.su0, 1)
    a.activation(T.zz[:, 1:2], T.ss[:, e + 1:e + 2], Act.Sqrt, scale=T.m1[:, 1:2]).then_inc(S.su1, 1)
    v.wait_ge(S.rd, 2)
    v.reciprocal(T.zz[:, 4:8], T.ss[:, e:e + 4]).then_inc(S.rc, 1)
    a.wait_ge(S.su0, 1)
    a.activation(T.rm[:, 0:HALF], T.ida[:, 0:HALF], Act.Identity, scale=T.zz[:, 0:1]).then_inc(S.r0, 1)
    a.wait_ge(S.su1, 1)
    a.activation(T.rm[:, HALF:TK], T.ida[:, HALF:TK], Act.Identity, scale=T.zz[:, 1:2]).then_inc(S.r1, 1)
    v.wait_ge(S.rc, 1)
    v.wait_ge(S.su0, 1)
    v.tensor_tensor_scan(T.lb0[:, 1:NP + 1], T.zz[:, 0:2 * NP:2], T.w1[:, 0:NP], T.zz[:, 0:1], mult, add).then_inc(
        S.l0, 1)
    v.wait_ge(S.su1, 1)
    v.tensor_tensor_scan(T.lb1[:, 1:NP + 1], T.zz[:, 1:2 * NP:2], T.w1[:, 0:NP], T.zz[:, 1:2], mult, add).then_inc(
        S.l1, 1)
    for b in range(4):
        if b == 0:
            pe.wait_ge(S.l0, 1)
            pe.wait_ge(S.r0, 1)
        if b == 2:
            pe.wait_ge(S.l1, 1)
            pe.wait_ge(S.r1, 1)
        lb = T.lb0 if b < 2 else T.lb1
        pe.matmul(T["ps%d" % b][:, 0:BL], lb[:, 4:4 + HALF], T.rm[:, BL * b:BL * b + BL], True, True).then_inc(
            S["bc%d" % b], 1)
    for b in range(4):
        v.wait_ge(S["bc%d" % b], 1)
        v.tensor_tensor(T.ys[:, BL * b:BL * b + BL], T.xs[:, BL * b:BL * b + BL], T["ps%d" % b][:, 0:BL],
                        mult).then_inc(S["ml%d" % b], 1)
    sy.wait_ge(S.ml0, 1)
    sy.wait_ge(S.ml1, 1)
    sy.dma_start(T.y[:, 0:HALF], T.ys[:, 0:HALF]).then_inc(S.st, 16)
    a.wait_ge(S.ml2, 1)
    a.dma_start(T.y[:, HALF:HALF + BL], T.ys[:, HALF:HALF + BL]).then_inc(S.st, 16)
    sy.wait_ge(S.ml3, 1)
    sy.dma_start(T.y[:, HALF + BL:TK], T.ys[:, HALF + BL:TK]).then_inc(S.st, 16)

    g.wait_ge(S.sent, 2 * E_HAND + E_RANK)
    sy.wait_ge(S.st, 48)
